import numpy as np
import ml_dtypes


def mxq(x, axis, fmt="e4m3"):
    dtype, down = {"e4m3": (ml_dtypes.float8_e4m3fn, 7), "e5m2": (ml_dtypes.float8_e5m2, 14)}[fmt]
    v = np.moveaxis(np.asarray(x, np.float32).astype(ml_dtypes.bfloat16).astype(np.float64), axis, -1)
    blocks = v.reshape(v.shape[:-1] + (-1, 32))
    amax = np.abs(blocks).max(-1, keepdims=True)
    byte = np.maximum(np.where(amax > 0, np.frexp(amax)[1] - 1 + 127, 0) - down, 1)
    scale = np.exp2(byte - 127.0)
    codes = (blocks / scale).astype(np.float32).astype(dtype).astype(np.float64)
    return np.moveaxis((codes * scale).reshape(v.shape), -1, axis)


WIDE = False


def mx_kscale(k):
    if not WIDE:
        return np.ones(k)
    levels = np.array([30, -30])
    if k % 512:
        return np.exp2(np.random.permutation(np.resize(levels, k // 32))).repeat(32)
    a = np.empty((k // 512, 16))
    for p in range(k // 512):
        a[p, :8] = np.random.permutation(np.resize(levels, 8))
        for g in range(8):
            far = levels[np.abs(levels - a[p, g]) >= 10]
            a[p, g + 8] = far[np.random.randint(len(far))]
    return np.exp2(a.ravel()).repeat(32)


def f64(x):
    return np.asarray(x).astype(np.float64)


def striped(idx):
    return np.tile(np.asarray(idx).reshape(-1, 16).T, (8, 1)).astype(np.uint16)


def unstriped(offs):
    return offs[:16].T.reshape(-1).astype(np.int64)


E2M1 = np.array([0.0, 0.5, 1.0, 1.5, 2.0, 3.0, 4.0, 6.0, -0.0, -0.5, -1.0, -1.5, -2.0, -3.0, -4.0, -6.0])


def pack_weight(w, fmt):
    k, n = w.shape
    w = f64(np.asarray(w, np.float32).astype(ml_dtypes.bfloat16)).reshape(k // 32, 32, n)
    amax = np.abs(w).max(1)
    if fmt in ("e4m3", "e5m2"):
        byte = np.frexp(amax)[1] - 1 + 127 - (7 if fmt == "e4m3" else 14)
    else:
        mant, ex = np.frexp(amax / 6.0)
        byte = np.where(mant > 0.5, ex, ex - 1) + 127
    byte = np.clip(np.where(amax > 0, byte, 1), 1, 254)
    scaled = (w * np.exp2(127.0 - byte)[:, None, :]).reshape(k, n).astype(np.float32)
    by_word = np.ascontiguousarray(scaled.reshape(k // 512, 128, 4, n).transpose(0, 1, 3, 2))
    if fmt in ("e4m3", "e5m2"):
        words = by_word.astype(ml_dtypes.float8_e4m3fn if fmt == "e4m3" else ml_dtypes.float8_e5m2).view(np.uint8)
    else:
        c = by_word.astype(ml_dtypes.float4_e2m1fn).view(np.uint8) & 0xF
        words = (c[..., 0::2] | (c[..., 1::2] << 4)).reshape(k // 512, 128, 2 * n)
    return np.ascontiguousarray(words), np.ascontiguousarray(byte.astype(np.uint8).reshape(k // 512, 16, n))


def unpack_weight(words, scales, fmt):
    g, _, n = scales.shape
    words = np.ascontiguousarray(words).reshape(g, 128, n, -1)
    if fmt in ("e4m3", "e5m2"):
        vals = words.view(ml_dtypes.float8_e4m3fn if fmt == "e4m3" else ml_dtypes.float8_e5m2).astype(np.float64)
    else:
        nib = np.empty((g, 128, n, 4), np.uint8)
        nib[..., 0::2] = words & 0xF
        nib[..., 1::2] = words >> 4
        vals = E2M1[nib]
    vals = vals * np.repeat(np.exp2(scales.astype(np.float64) - 127.0), 8, axis=1)[..., None]
    return vals.transpose(0, 1, 3, 2).reshape(g * 512, n)


def e4m3fn_bytes(y):
    return np.clip(np.asarray(y, np.float64), -448.0, 448.0).astype(np.float32).astype(ml_dtypes.float8_e4m3fn).view(np.uint8)


def e4m3fn_values(b):
    return np.asarray(b, np.uint8).view(ml_dtypes.float8_e4m3fn).astype(np.float64)


K, T, J, R, V, U, C, N = 512, 1024, 256, 512, 1024, 256, 512, 256


def setup_inputs():
    n = np.random.standard_normal
    idx = np.random.permutation(T)[:J]
    idx2 = np.random.permutation(V)[:U]
    fk = mx_kscale(K)
    fr = mx_kscale(R)
    xtp = pack_weight(n((K, T)) / fk[:, None], "e4m3")
    wp = pack_weight(n((K, R)) * 1 / np.sqrt(K) * fk[:, None] * fr, "e2m1")
    wbp = pack_weight(n((R, N)) * 1 / np.sqrt(R) / fr[:, None], "e5m2")
    return {
        "xt_words": xtp[0],
        "xt_scales": xtp[1],
        "w_words": wp[0],
        "w_scales": wp[1],
        "ca": e4m3fn_bytes(60.0 * n((R, V))),
        "st": (np.random.uniform(0.008, 0.024, (R, 1)) * fr[:, None]).astype(np.float32),
        "wb_words": wbp[0],
        "wb_scales": wbp[1],
        "offs": striped(idx),
        "offs2": striped(idx2),
    }


def reference(xt_words, xt_scales, w_words, w_scales, ca, st, wb_words, wb_scales, offs, offs2):
    idx = unstriped(offs)
    idx2 = unstriped(offs2)
    xtu = unpack_weight(xt_words, xt_scales, "e4m3")
    wu = unpack_weight(w_words, w_scales, "e2m1")
    wbu = unpack_weight(wb_words, wb_scales, "e5m2")
    xtidxg = xtu[:, idx]
    a = wu.T @ xtidxg
    g1 = e4m3fn_values(ca)[:, idx2] * f64(st)
    h1 = np.maximum(a, 0.0)
    hid = np.concatenate([h1, g1], axis=1)
    hidq = mxq(hid, 0, "e4m3")
    p = wbu.T @ hidq
    return p

from contextlib import ExitStack

import concourse.mybir as mybir

K, T, J, R, V, U, C, N = 512, 1024, 256, 512, 1024, 256, 512, 256
FLOPS = 2 * K * R * J + 2 * R * N * C

F32 = mybir.dt.float32
BF16 = mybir.dt.bfloat16
I32 = mybir.dt.int32
U32 = mybir.dt.uint32
U16 = mybir.dt.uint16
U8 = mybir.dt.uint8
E4M3 = mybir.dt.float8_e4m3fn
E4M3X4 = mybir.dt.float8_e4m3fn_x4
E5M2X4 = mybir.dt.float8_e5m2_x4
E2M1X4 = mybir.dt.float4_e2m1fn_x4
ACT = mybir.ActivationFunctionType

P = 128
PACK = 4


def load_scale_rows(queue, plane, rows, q):
    queue.dma_start(out=plane[32 * q : 32 * q + 4, :].bitcast(I32), in_=rows[0, 4 * q : 4 * q + 4, :].bitcast(I32))


def tile_list_appended_kernel(tc, xt_words, xt_scales, w_words, w_scales, ca, st, wb_words, wb_scales, offs, offs2, out):
    nc = tc.nc
    with ExitStack() as ctx:
        keep = ctx.enter_context(tc.tile_pool(name="keep", bufs=1))
        psum = ctx.enter_context(tc.psum_pool(name="psum", bufs=1))

        list1 = keep.tile([P, J // 16], U16)
        list2 = keep.tile([P, U // 16], U16)
        xw = keep.tile([P, T], U32, align_bytes=64)
        xs = keep.tile([P, T], U8, tag="xs_then_hid_b", align_bytes=64)
        ww_raw = keep.tile([P, R], U16, tag="ww_then_stored", align_bytes=64)
        ws_raw = keep.tile([P, R], U8, align_bytes=64)
        wbw = keep.tile([P, N], U32, align_bytes=64)
        wbs = keep.tile([P, N], U8, align_bytes=64)
        step = keep.tile([P, PACK], F32)
        store = [keep.tile([P, V], U8, name=f"store{t}", align_bytes=64) for t in range(PACK)]
        ca_rows = ca.rearrange("(p t) v -> t p v", t=PACK)

        nc.vector.memset(ws_raw[:].bitcast(I32), 0)
        nc.vector.memset(xs[:].bitcast(I32), 0)
        nc.vector.memset(wbs[:].bitcast(I32), 0)

        nc.sync.dma_start(list2[:], offs2)
        for t in range(3):
            nc.sync.dma_start(out=store[t][:], in_=ca_rows[t])
        nc.sync.dma_start(list1[:], offs)
        nc.sync.dma_start(out=store[3][:], in_=ca_rows[3])
        nc.sync.dma_start(out=ww_raw[:].bitcast(I32), in_=w_words[0].bitcast(I32))
        nc.sync.dma_start(out=xw[:].bitcast(I32), in_=xt_words[0].rearrange("p n t -> p (n t)").bitcast(I32))
        nc.gpsimd.dma_start(out=step[:], in_=st.rearrange("(p t) o -> p (t o)", t=PACK))
        load_scale_rows(nc.gpsimd, ws_raw, w_scales, 3)
        for q in range(3):
            load_scale_rows(nc.sync, ws_raw, w_scales, q)
        for q in range(4):
            load_scale_rows(nc.sync, xs, xt_scales, q)
        nc.sync.dma_start(out=wbw[:].bitcast(I32), in_=wb_words[0].rearrange("p n t -> p (n t)").bitcast(I32))
        for q in range(4):
            load_scale_rows(nc.sync, wbs, wb_scales, q)

        picked = [keep.tile([P, U], U8, name=f"picked{t}", align_bytes=64) for t in range(PACK)]
        stored = keep.tile([P, PACK, U], F32, tag="ww_then_stored", align_bytes=64)

        def look_up(t):
            nc.vector.tensor_copy(picked[t][:], store[t][:].indirect(list2[:]))
            nc.scalar.activation(out=stored[:, t, :], in_=picked[t][:].bitcast(E4M3), func=ACT.Copy, scale=step[:, t : t + 1])

        ww = keep.tile([P, R], U16, align_bytes=64)
        nc.scalar.copy(
            out=ww[:].rearrange("p (t a m) -> p a t m", t=PACK, m=8),
            in_=ww_raw[:].rearrange("p (a m t) -> p a t m", t=PACK, m=8),
        )
        for t in range(PACK):
            look_up(t)
        ws = keep.tile([P, R], U8, align_bytes=64)
        nc.gpsimd.tensor_copy(
            out=ws[:].rearrange("p (t a m) -> p a t m", t=PACK, m=16),
            in_=ws_raw[:].rearrange("p (a m t) -> p a t m", t=PACK, m=16),
        )

        half = J // 2
        xwg = keep.tile([P, J], U32, align_bytes=64)
        nc.vector.tensor_copy(xwg[:], xw[:].indirect(list1[:]))
        first = []
        for h in range(2):
            xsg = keep.tile([P, half], U8, name=f"xsg{h}", align_bytes=64)
            nc.vector.tensor_copy(xsg[:], xs[:].indirect(list1[:, h * half // 16 : (h + 1) * half // 16]))
            acc = psum.tile([P, PACK, half], F32, name=f"first{h}")
            for t in range(PACK):
                nc.tensor.matmul_mx(
                    out=acc[:, t, :],
                    lhsT=ww[:, t * P : (t + 1) * P].bitcast(E2M1X4),
                    lhsT_scale=ws[:, t * P : (t + 1) * P],
                    rhs=xwg[:, h * half : (h + 1) * half].bitcast(E4M3X4),
                    rhs_scale=xsg[:],
                    start=True,
                    stop=True,
                )
            first.append(acc)

        out_rows = out.rearrange("(h p) c -> p h c", p=P)

        def quantise(name, hid, width):
            codes = keep.tile([P, width], U32, name=f"codes_{name}", align_bytes=64)
            scales = keep.tile([P, width], U8, name=f"scales_{name}", align_bytes=64)
            nc.vector.quantize_mx(out=codes[:].bitcast(E4M3X4), scales=scales[:], in_=hid[:].rearrange("p c t -> p (c t)"))
            return codes, scales

        def second(res, h, codes, scales):
            nc.tensor.matmul_mx(
                out=res,
                lhsT=wbw[:, h * P : (h + 1) * P].bitcast(E5M2X4),
                lhsT_scale=wbs[:, h * P : (h + 1) * P],
                rhs=codes[:].bitcast(E4M3X4),
                rhs_scale=scales[:],
                start=True,
                stop=True,
            )

        hid_b = keep.tile([P, U, PACK], BF16, tag="xs_then_hid_b", align_bytes=64)
        nc.vector.tensor_copy(out=hid_b[:], in_=stored[:].rearrange("p t u -> p u t"))
        hid_a = [keep.tile([P, half, PACK], BF16, name=f"hid_a{h}", align_bytes=64) for h in range(2)]
        for h in range(2):
            nc.scalar.activation(out=hid_a[h][:], in_=first[h][:].rearrange("p t j -> p j t"), func=ACT.Relu)

        quant_b = quantise("b", hid_b, U)
        res_b = psum.tile([P, 2, U], F32)
        for h in range(2):
            second(res_b[:, h, :], h, *quant_b)
        done_b = keep.tile([P, 2, U], F32)
        nc.scalar.copy(out=done_b[:], in_=res_b[:])
        nc.sync.dma_start(out=out_rows[:, :, J:C], in_=done_b[:])

        quant_a0 = quantise("a0", hid_a[0], half)
        quant_a1 = quantise("a1", hid_a[1], half)
        res_a0 = psum.tile([P, 2, half], F32)
        for h in range(2):
            second(res_a0[:, h, :], h, *quant_a0)
        done_a0 = keep.tile([P, 2, half], F32)
        nc.vector.tensor_copy(out=done_a0[:], in_=res_a0[:])
        nc.sync.dma_start(out=out_rows[:, :, 0:half], in_=done_a0[:])

        for h, copy, queue in ((0, nc.scalar.copy, nc.scalar), (1, nc.vector.tensor_copy, nc.sync)):
            res = psum.tile([P, half], F32, name=f"res_a1{h}")
            second(res[:], h, *quant_a1)
            done = keep.tile([P, half], F32, name=f"done_a1{h}")
            copy(out=done[:], in_=res[:])
            queue.dma_start(out=out_rows[:, h, half:J], in_=done[:])
